import numpy as np
import ml_dtypes


def mxq(x, axis, fmt="e4m3"):
    dtype, down = {"e4m3": (ml_dtypes.float8_e4m3fn, 7), "e5m2": (ml_dtypes.float8_e5m2, 14)}[fmt]
    v = np.moveaxis(np.asarray(x, np.float32).astype(ml_dtypes.bfloat16).astype(np.float64), axis, -1)
    blocks = v.reshape(v.shape[:-1] + (-1, 32))
    amax = np.abs(blocks).max(-1, keepdims=True)
    byte = np.maximum(np.where(amax > 0, np.frexp(amax)[1] - 1 + 127, 0) - down, 1)
    scale = np.exp2(byte - 127.0)
    codes = (blocks / scale).astype(np.float32).astype(dtype).astype(np.float64)
    return np.moveaxis((codes * scale).reshape(v.shape), -1, axis)


WIDE = False


def mx_kscale(k):
    if not WIDE:
        return np.ones(k)
    levels = np.array([30, -30])
    if k % 512:
        return np.exp2(np.random.permutation(np.resize(levels, k // 32))).repeat(32)
    a = np.empty((k // 512, 16))
    for p in range(k // 512):
        a[p, :8] = np.random.permutation(np.resize(levels, 8))
        for g in range(8):
            far = levels[np.abs(levels - a[p, g]) >= 10]
            a[p, g + 8] = far[np.random.randint(len(far))]
    return np.exp2(a.ravel()).repeat(32)


def f64(x):
    return np.asarray(x).astype(np.float64)


def striped(idx):
    return np.tile(np.asarray(idx).reshape(-1, 16).T, (8, 1)).astype(np.uint16)


def unstriped(offs):
    return offs[:16].T.reshape(-1).astype(np.int64)


E2M1 = np.array([0.0, 0.5, 1.0, 1.5, 2.0, 3.0, 4.0, 6.0, -0.0, -0.5, -1.0, -1.5, -2.0, -3.0, -4.0, -6.0])


def pack_weight(w, fmt):
    k, n = w.shape
    w = f64(np.asarray(w, np.float32).astype(ml_dtypes.bfloat16)).reshape(k // 32, 32, n)
    amax = np.abs(w).max(1)
    if fmt == "e4m3":
        byte = np.frexp(amax)[1] - 1 + 127 - 7
    else:
        mant, ex = np.frexp(amax / 6.0)
        byte = np.where(mant > 0.5, ex, ex - 1) + 127
    byte = np.clip(np.where(amax > 0, byte, 1), 1, 254)
    scaled = (w * np.exp2(127.0 - byte)[:, None, :]).reshape(k, n).astype(np.float32)
    by_word = np.ascontiguousarray(scaled.reshape(k // 512, 128, 4, n).transpose(0, 1, 3, 2))
    if fmt == "e4m3":
        words = by_word.astype(ml_dtypes.float8_e4m3fn).view(np.uint8)
    else:
        c = by_word.astype(ml_dtypes.float4_e2m1fn).view(np.uint8) & 0xF
        words = (c[..., 0::2] | (c[..., 1::2] << 4)).reshape(k // 512, 128, 2 * n)
    return np.ascontiguousarray(words), np.ascontiguousarray(byte.astype(np.uint8).reshape(k // 512, 16, n))


def unpack_weight(words, scales, fmt):
    g, _, n = scales.shape
    words = np.ascontiguousarray(words).reshape(g, 128, n, -1)
    if fmt == "e4m3":
        vals = words.view(ml_dtypes.float8_e4m3fn).astype(np.float64)
    else:
        nib = np.empty((g, 128, n, 4), np.uint8)
        nib[..., 0::2] = words & 0xF
        nib[..., 1::2] = words >> 4
        vals = E2M1[nib]
    vals = vals * np.repeat(np.exp2(scales.astype(np.float64) - 127.0), 8, axis=1)[..., None]
    return vals.transpose(0, 1, 3, 2).reshape(g * 512, n)


K, F, T, Z, J, R, O, N, E = 512, 512, 1024, 1024, 256, 512, 256, 256, 1024


def setup_inputs():
    n = np.random.standard_normal
    idx = np.random.permutation(T)[:J]
    idx2 = np.random.permutation(Z)[:J]
    idx3 = np.random.permutation(J)[:O]
    idx4 = np.random.permutation(O)[:O]
    idx5 = np.random.permutation(T)[:O]
    idx6 = np.random.permutation(E)[:O]
    fk = mx_kscale(K)
    fr = mx_kscale(R)
    ff = mx_kscale(F)
    xtp = pack_weight(n((K, T)) / fk[:, None], "e2m1")
    wp = pack_weight(n((K, R)) * 1 / np.sqrt(K) * fk[:, None] * fr, "e4m3")
    xop = pack_weight(n((F, Z)) / ff[:, None], "e4m3")
    w0p = pack_weight(n((F, R)) * 1 / np.sqrt(F) * ff[:, None] * fr, "e2m1")
    wbp = pack_weight(n((R, N)) * 1 / np.sqrt(R) / fr[:, None], "e2m1")
    wsp = pack_weight(n((K, N)) * 1 / np.sqrt(K) * fk[:, None], "e4m3")
    return {
        "xt_words": xtp[0],
        "xt_scales": xtp[1],
        "w_words": wp[0],
        "w_scales": wp[1],
        "xo_words": xop[0],
        "xo_scales": xop[1],
        "w0_words": w0p[0],
        "w0_scales": w0p[1],
        "wb_words": wbp[0],
        "wb_scales": wbp[1],
        "ws_words": wsp[0],
        "ws_scales": wsp[1],
        "tz": (n((N, E))).astype(np.float32),
        "offs": striped(idx),
        "offs2": striped(idx2),
        "offs3": striped(idx3),
        "offs4": striped(idx4),
        "offs5": striped(idx5),
        "offs6": striped(idx6),
    }


def reference(xt_words, xt_scales, w_words, w_scales, xo_words, xo_scales, w0_words, w0_scales, wb_words, wb_scales, ws_words, ws_scales, tz, offs, offs2, offs3, offs4, offs5, offs6):
    idx = unstriped(offs)
    idx2 = unstriped(offs2)
    idx3 = unstriped(offs3)
    idx4 = unstriped(offs4)
    idx5 = unstriped(offs5)
    idx6 = unstriped(offs6)
    xtu = unpack_weight(xt_words, xt_scales, "e2m1")
    wu = unpack_weight(w_words, w_scales, "e4m3")
    xou = unpack_weight(xo_words, xo_scales, "e4m3")
    w0u = unpack_weight(w0_words, w0_scales, "e2m1")
    wbu = unpack_weight(wb_words, wb_scales, "e2m1")
    wsu = unpack_weight(ws_words, ws_scales, "e4m3")
    xtidxg = xtu[:, idx]
    xoidx2g = xou[:, idx2]
    a = wu.T @ xtidxg + w0u.T @ xoidx2g
    ca = a[:, idx3]
    hid = np.abs(ca - ca[:, idx4])
    hidq = mxq(hid, 0, "e5m2")
    xtidx5g = xtu[:, idx5]
    p = wbu.T @ hidq + wsu.T @ xtidx5g
    y = p + f64(tz)[:, idx6]
    return y

@@ -1,0 +1,177 @@
+from contextlib import ExitStack
+
+import concourse.mybir as mybir
+
+F32 = mybir.dt.float32
+BF16 = mybir.dt.bfloat16
+I32 = mybir.dt.int32
+U32 = mybir.dt.uint32
+U16 = mybir.dt.uint16
+U8 = mybir.dt.uint8
+E4M3 = mybir.dt.float8_e4m3fn_x4
+E5M2 = mybir.dt.float8_e5m2_x4
+E2M1 = mybir.dt.float4_e2m1fn_x4
+ALU = mybir.AluOpType
+ACT = mybir.ActivationFunctionType
+
+P = 128
+PACK = 4
+K, T, Z, J, R, O, N, E = 512, 1024, 1024, 256, 512, 256, 256, 1024
+FLOPS = 2 * (2 * K * R * J + R * N * O + K * N * O)
+WINDOW = 352
+SCALAR_PLACES = 128
+
+
+def tile_list_neighbours_bank_further_tabled_kernel(
+    tc, xt_words, xt_scales, w_words, w_scales, xo_words, xo_scales, w0_words, w0_scales,
+    wb_words, wb_scales, ws_words, ws_scales, tz, offs, offs2, offs3, offs4, offs5, offs6, out,
+):
+    nc = tc.nc
+    with ExitStack() as ctx:
+        sb = ctx.enter_context(tc.tile_pool(name="sb", bufs=1))
+        ps = ctx.enter_context(tc.psum_pool(name="ps", bufs=1))
+
+        def new(name, shape, dtype, tag=""):
+            return sb.tile(shape, dtype, name=name, tag=tag, align_bytes=64)
+
+        def load_list(name, src):
+            tile = sb.tile([P, 16], U16, name=name)
+            nc.sync.dma_start(tile[:], src)
+            return tile
+
+        def load_words(queue, name, src, cols, dtype):
+            tile = new(name, [P, cols], dtype)
+            queue.dma_start(tile[:].bitcast(I32), src.bitcast(I32))
+            return tile
+
+        def load_scales(queue, tile, src, quadrants=range(4)):
+            for q in quadrants:
+                rows = src[0, 4 * q : 4 * q + 4, :].bitcast(I32)
+                queue.dma_start(tile[32 * q : 32 * q + 32, :].bitcast(I32), rows.unsqueeze(0).broadcast_to([8] + list(rows.shape)))
+
+        xt_s, xo_s = new("xt_s", [P, T], U8), new("xo_s", [P, Z], U8)
+        w_s, w0_s = new("w_s", [P, R], U8), new("w0_s", [P, R], U8)
+        ws_s, wb_s = new("ws_s", [P, N], U8), new("wb_s", [P, N], U8)
+
+        def fp8_rows(words):
+            return words[0].rearrange("p n t -> p (n t)")
+
+        def load_tz(m):
+            tile = new(f"tz{m}", [P, E], F32)
+            nc.sync.dma_start(tile[:], tz[m * P : (m + 1) * P, :])
+            return tile
+
+        load_scales(nc.gpsimd, w0_s, w0_scales, range(2))
+        list1 = load_list("list1", offs)
+        load_scales(nc.scalar, xt_s, xt_scales, range(3))
+        load_scales(nc.sync, xt_s, xt_scales, range(3, 4))
+        list5 = load_list("list5", offs5)
+        xt_w = load_words(nc.sync, "xt_w", xt_words[0], T, U16)
+        w_w = load_words(nc.sync, "w_w", fp8_rows(w_words), R, U32)
+        load_scales(nc.sync, w_s, w_scales)
+        list2 = load_list("list2", offs2)
+        load_scales(nc.sync, xo_s, xo_scales, range(1))
+        xo_w = load_words(nc.sync, "xo_w", fp8_rows(xo_words), Z, U32)
+        w0_w = load_words(nc.sync, "w0_w", w0_words[0], R, U16)
+        load_scales(nc.sync, xo_s, xo_scales, range(1, 4))
+        load_scales(nc.sync, w0_s, w0_scales, range(2, 4))
+        list3 = load_list("list3", offs3)
+        list4 = load_list("list4", offs4)
+        list6 = load_list("list6", offs6)
+        tz_sb = [load_tz(0)]
+        ws_w = load_words(nc.sync, "ws_w", fp8_rows(ws_words), N, U32)
+        wb_w = load_words(nc.sync, "wb_w", wb_words[0], N, U16)
+        load_scales(nc.sync, ws_s, ws_scales)
+        tz_sb.append(load_tz(1))
+        load_scales(nc.sync, wb_s, wb_scales)
+
+        def deal(engine_copy, name, src, dtype, line):
+            dealt = new(name, [P, PACK, P], dtype)
+            engine_copy(
+                dealt[:].rearrange("p t (c i) -> p c t i", i=line),
+                src[:].rearrange("p (c i t) -> p c t i", i=line, t=PACK),
+            )
+            return dealt
+
+        def pick(name, src, offsets, dtype):
+            picked = new(name, [P, J], dtype)
+            nc.vector.tensor_copy(picked[:], src[:].indirect(offsets[:]))
+            return picked
+
+        xt1_s = pick("xt1_s", xt_s, list1, U8)
+        xt1_w = pick("xt1_w", xt_w, list1, U16)
+        w_sd = deal(nc.vector.tensor_copy, "w_sd", w_s, U8, 16)
+        w_wd = deal(nc.scalar.copy, "w_wd", w_w, U32, 4)
+        w0_wd = deal(nc.scalar.copy, "w0_wd", w0_w, U16, 8)
+        xo2_w = pick("xo2_w", xo_w, list2, U32)
+        xo2_s = pick("xo2_s", xo_s, list2, U8)
+        w0_sd = deal(nc.gpsimd.tensor_copy, "w0_sd", w0_s, U8, 16)
+
+        a_ps = [ps.tile([P, J], F32, name=f"a_ps{t}") for t in range(PACK)]
+        for t in range(PACK):
+            nc.tensor.matmul_mx(a_ps[t][:], lhsT=w_wd[:, t, :].bitcast(E4M3), lhsT_scale=w_sd[:, t, :],
+                                rhs=xt1_w[:].bitcast(E2M1), rhs_scale=xt1_s[:], start=True, stop=False)
+        for t in range(PACK):
+            nc.tensor.matmul_mx(a_ps[t][:], lhsT=w0_wd[:, t, :].bitcast(E2M1), lhsT_scale=w0_sd[:, t, :],
+                                rhs=xo2_w[:].bitcast(E4M3), rhs_scale=xo2_s[:], start=False, stop=True)
+
+        xt5_s = pick("xt5_s", xt_s, list5, U8)
+        xt5_w = pick("xt5_w", xt_w, list5, U16)
+        p_ps = [ps.tile([P, O], F32, name=f"p_ps{m}") for m in range(2)]
+        for m in range(2):
+            rows = slice(m * P, (m + 1) * P)
+            nc.tensor.matmul_mx(p_ps[m][:], lhsT=ws_w[:, rows].bitcast(E4M3), lhsT_scale=ws_s[:, rows],
+                                rhs=xt5_w[:].bitcast(E2M1), rhs_scale=xt5_s[:], start=True, stop=False)
+
+        def scalar_copy(dst, src):
+            nc.scalar.activation(dst, src, ACT.Copy)
+
+        vector_copy = nc.vector.tensor_copy
+        a_sb = [new(f"a{t}", [P, WINDOW], F32, tag=f"a{t}") for t in range(PACK)]
+        ca = [new(f"ca{t}", [P, WINDOW], F32) for t in range(PACK)]
+        cb = [new(f"cb{t}", [P, O], F32, tag=f"cb{t}") for t in range(PACK)]
+        diff = new("diff", [P, PACK, O], F32)
+        hid = new("hid", [P, O, PACK], BF16)
+
+        def evacuate(copy, t):
+            copy(a_sb[t][:, :J], a_ps[t][:])
+
+        def take_slots(copy, t):
+            copy(ca[t][:, :O], a_sb[t][:].indirect(list3[:]))
+
+        def take_neighbours(copy, t):
+            copy(cb[t][:], ca[t][:].indirect(list4[:]))
+
+        def subtract(engine, t):
+            engine.tensor_tensor(diff[:, t, :], ca[t][:, :O], cb[t][:], ALU.subtract)
+
+        def take_entries(m, tag):
+            taken = new(f"tz6_{m}", [P, O], F32, tag=tag)
+            scalar_copy(taken[:], tz_sb[m][:].indirect(list6[:]))
+            return taken
+
+        for t in range(PACK):
+            evacuate(scalar_copy, t)
+        for take in (take_slots, take_neighbours):
+            for t in range(PACK):
+                take(vector_copy if t < 2 else scalar_copy, t)
+        for t in range(PACK):
+            subtract(nc.vector, t)
+        tz6 = [take_entries(0, "a3")]
+
+        woven = diff[:].rearrange("p t o -> p o t")
+        nc.scalar.activation(hid[:, :SCALAR_PLACES, :], woven[:, :SCALAR_PLACES, :], ACT.Abs)
+        rest = woven[:, SCALAR_PLACES:, :]
+        nc.vector.scalar_tensor_tensor(hid[:, SCALAR_PLACES:, :], rest, -1.0, rest, ALU.mult, ALU.max)
+        tz6.append(take_entries(1, "cb3"))
+
+        hid_w = new("hid_w", [P, O], U32)
+        hid_s = new("hid_s", [P, O], U8)
+        nc.vector.quantize_mx(hid_w[:].bitcast(E5M2), hid_s[:], hid[:].rearrange("p o t -> p (o t)"))
+        for m in range(2):
+            rows = slice(m * P, (m + 1) * P)
+            nc.tensor.matmul_mx(p_ps[m][:], lhsT=wb_w[:, rows].bitcast(E2M1), lhsT_scale=wb_s[:, rows],
+                                rhs=hid_w[:].bitcast(E5M2), rhs_scale=hid_s[:], start=False, stop=True)
+            res = new(f"res{m}", [P, O], F32)
+            nc.vector.tensor_tensor(res[:], p_ps[m][:], tz6[m][:], ALU.add)
+            nc.sync.dma_start(out[rows, :], res[:])

@@ -46,12 +46,21 @@ def tile_list_neighbours_bank_further_tabled_kernel(
 
         def load_scales(queue, tile, src, quadrants=range(4)):
             for q in quadrants:
+                queue.dma_start(tile[32 * q : 32 * q + 4, :].bitcast(I32), src[0, 4 * q : 4 * q + 4, :].bitcast(I32))
+
+        def load_scales_repeated(queue, tile, src, quadrants=range(4)):
+            for q in quadrants:
                 rows = src[0, 4 * q : 4 * q + 4, :].bitcast(I32)
                 queue.dma_start(tile[32 * q : 32 * q + 32, :].bitcast(I32), rows.unsqueeze(0).broadcast_to([8] + list(rows.shape)))
 
-        xt_s, xo_s = new("xt_s", [P, T], U8), new("xo_s", [P, Z], U8)
-        w_s, w0_s = new("w_s", [P, R], U8), new("w0_s", [P, R], U8)
-        ws_s, wb_s = new("ws_s", [P, N], U8), new("wb_s", [P, N], U8)
+        def zeroed_plane(name, cols):
+            tile = new(name, [P, cols], U8)
+            nc.vector.memset(tile[:].bitcast(I32), 0)
+            return tile
+
+        xt_s, w0_s = new("xt_s", [P, T], U8), new("w0_s", [P, R], U8)
+        w_s, xo_s = zeroed_plane("w_s", R), zeroed_plane("xo_s", Z)
+        ws_s, wb_s = zeroed_plane("ws_s", N), zeroed_plane("wb_s", N)
 
         def fp8_rows(words):
             return words[0].rearrange("p n t -> p (n t)")
@@ -61,24 +70,23 @@ def tile_list_neighbours_bank_further_tabled_kernel(
             nc.sync.dma_start(tile[:], tz[m * P : (m + 1) * P, :])
             return tile
 
-        load_scales(nc.gpsimd, w0_s, w0_scales, range(2))
+        load_scales_repeated(nc.gpsimd, w0_s, w0_scales, range(2))
         list1 = load_list("list1", offs)
-        load_scales(nc.scalar, xt_s, xt_scales, range(3))
-        load_scales(nc.sync, xt_s, xt_scales, range(3, 4))
-        list5 = load_list("list5", offs5)
+        load_scales_repeated(nc.scalar, xt_s, xt_scales, range(3))
+        load_scales_repeated(nc.sync, xt_s, xt_scales, range(3, 4))
+        list2 = load_list("list2", offs2)
         xt_w = load_words(nc.sync, "xt_w", xt_words[0], T, U16)
         w_w = load_words(nc.sync, "w_w", fp8_rows(w_words), R, U32)
         load_scales(nc.sync, w_s, w_scales)
-        list2 = load_list("list2", offs2)
-        load_scales(nc.sync, xo_s, xo_scales, range(1))
+        load_scales_repeated(nc.sync, w0_s, w0_scales, range(2, 4))
         xo_w = load_words(nc.sync, "xo_w", fp8_rows(xo_words), Z, U32)
         w0_w = load_words(nc.sync, "w0_w", w0_words[0], R, U16)
-        load_scales(nc.sync, xo_s, xo_scales, range(1, 4))
-        load_scales(nc.sync, w0_s, w0_scales, range(2, 4))
+        load_scales(nc.sync, xo_s, xo_scales)
+        list5 = load_list("list5", offs5)
         list3 = load_list("list3", offs3)
+        tz_sb = [load_tz(0)]
         list4 = load_list("list4", offs4)
         list6 = load_list("list6", offs6)
-        tz_sb = [load_tz(0)]
         ws_w = load_words(nc.sync, "ws_w", fp8_rows(ws_words), N, U32)
         wb_w = load_words(nc.sync, "wb_w", wb_words[0], N, U16)
         load_scales(nc.sync, ws_s, ws_scales)
@@ -103,9 +111,9 @@ def tile_list_neighbours_bank_further_tabled_kernel(
         w_sd = deal(nc.vector.tensor_copy, "w_sd", w_s, U8, 16)
         w_wd = deal(nc.scalar.copy, "w_wd", w_w, U32, 4)
         w0_wd = deal(nc.scalar.copy, "w0_wd", w0_w, U16, 8)
+        w0_sd = deal(nc.vector.tensor_copy, "w0_sd", w0_s, U8, 16)
         xo2_w = pick("xo2_w", xo_w, list2, U32)
         xo2_s = pick("xo2_s", xo_s, list2, U8)
-        w0_sd = deal(nc.gpsimd.tensor_copy, "w0_sd", w0_s, U8, 16)
 
         a_ps = [ps.tile([P, J], F32, name=f"a_ps{t}") for t in range(PACK)]
         for t in range(PACK):
@@ -160,7 +168,11 @@ def tile_list_neighbours_bank_further_tabled_kernel(
         tz6 = [take_entries(0, "a3")]
 
         woven = diff[:].rearrange("p t o -> p o t")
-        nc.scalar.activation(hid[:, :SCALAR_PLACES, :], woven[:, :SCALAR_PLACES, :], ACT.Abs)
+        nc.scalar.activation(
+            hid[:, :SCALAR_PLACES, :].rearrange("p (c i) t -> p c t i", i=4),
+            diff[:, :, :SCALAR_PLACES].rearrange("p t (c i) -> p c t i", i=4),
+            ACT.Abs,
+        )
         rest = woven[:, SCALAR_PLACES:, :]
         nc.vector.scalar_tensor_tensor(hid[:, SCALAR_PLACES:, :], rest, -1.0, rest, ALU.mult, ALU.max)
         tz6.append(take_entries(1, "cb3"))

@@ -58,8 +58,8 @@ def tile_list_neighbours_bank_further_tabled_kernel(
             nc.vector.memset(tile[:].bitcast(I32), 0)
             return tile
 
-        xt_s, w0_s = new("xt_s", [P, T], U8), new("w0_s", [P, R], U8)
-        w_s, xo_s = zeroed_plane("w_s", R), zeroed_plane("xo_s", Z)
+        xt_s, xo_s = new("xt_s", [P, T], U8), new("xo_s", [P, Z], U8)
+        w_s, w0_s = zeroed_plane("w_s", R), zeroed_plane("w0_s", R)
         ws_s, wb_s = zeroed_plane("ws_s", N), zeroed_plane("wb_s", N)
 
         def fp8_rows(words):
@@ -70,18 +70,18 @@ def tile_list_neighbours_bank_further_tabled_kernel(
             nc.sync.dma_start(tile[:], tz[m * P : (m + 1) * P, :])
             return tile
 
-        load_scales_repeated(nc.gpsimd, w0_s, w0_scales, range(2))
+        xo_w = load_words(nc.gpsimd, "xo_w", fp8_rows(xo_words), Z, U32)
+        load_scales_repeated(nc.gpsimd, xo_s, xo_scales, range(2))
         list1 = load_list("list1", offs)
         load_scales_repeated(nc.scalar, xt_s, xt_scales, range(3))
         load_scales_repeated(nc.sync, xt_s, xt_scales, range(3, 4))
-        list2 = load_list("list2", offs2)
         xt_w = load_words(nc.sync, "xt_w", xt_words[0], T, U16)
         w_w = load_words(nc.sync, "w_w", fp8_rows(w_words), R, U32)
+        list2 = load_list("list2", offs2)
         load_scales(nc.sync, w_s, w_scales)
-        load_scales_repeated(nc.sync, w0_s, w0_scales, range(2, 4))
-        xo_w = load_words(nc.sync, "xo_w", fp8_rows(xo_words), Z, U32)
+        load_scales_repeated(nc.sync, xo_s, xo_scales, range(2, 4))
         w0_w = load_words(nc.sync, "w0_w", w0_words[0], R, U16)
-        load_scales(nc.sync, xo_s, xo_scales)
+        load_scales(nc.sync, w0_s, w0_scales)
         list5 = load_list("list5", offs5)
         list3 = load_list("list3", offs3)
         tz_sb = [load_tz(0)]
@@ -111,9 +111,9 @@ def tile_list_neighbours_bank_further_tabled_kernel(
         w_sd = deal(nc.vector.tensor_copy, "w_sd", w_s, U8, 16)
         w_wd = deal(nc.scalar.copy, "w_wd", w_w, U32, 4)
         w0_wd = deal(nc.scalar.copy, "w0_wd", w0_w, U16, 8)
-        w0_sd = deal(nc.vector.tensor_copy, "w0_sd", w0_s, U8, 16)
         xo2_w = pick("xo2_w", xo_w, list2, U32)
         xo2_s = pick("xo2_s", xo_s, list2, U8)
+        w0_sd = deal(nc.vector.tensor_copy, "w0_sd", w0_s, U8, 16)
 
         a_ps = [ps.tile([P, J], F32, name=f"a_ps{t}") for t in range(PACK)]
         for t in range(PACK):

@@ -19,7 +19,7 @@ PACK = 4
 K, T, Z, J, R, O, N, E = 512, 1024, 1024, 256, 512, 256, 256, 1024
 FLOPS = 2 * (2 * K * R * J + R * N * O + K * N * O)
 WINDOW = 352
-SCALAR_PLACES = 128
+HALF = O // 2
 
 
 def tile_list_neighbours_bank_further_tabled_kernel(
@@ -71,15 +71,15 @@ def tile_list_neighbours_bank_further_tabled_kernel(
             return tile
 
         xo_w = load_words(nc.gpsimd, "xo_w", fp8_rows(xo_words), Z, U32)
-        load_scales_repeated(nc.gpsimd, xo_s, xo_scales, range(2))
+        w_w = load_words(nc.gpsimd, "w_w", fp8_rows(w_words), R, U32)
+        load_scales_repeated(nc.gpsimd, xo_s, xo_scales, range(1))
         list1 = load_list("list1", offs)
         load_scales_repeated(nc.scalar, xt_s, xt_scales, range(3))
         load_scales_repeated(nc.sync, xt_s, xt_scales, range(3, 4))
         xt_w = load_words(nc.sync, "xt_w", xt_words[0], T, U16)
-        w_w = load_words(nc.sync, "w_w", fp8_rows(w_words), R, U32)
         list2 = load_list("list2", offs2)
         load_scales(nc.sync, w_s, w_scales)
-        load_scales_repeated(nc.sync, xo_s, xo_scales, range(2, 4))
+        load_scales_repeated(nc.sync, xo_s, xo_scales, range(1, 4))
         w0_w = load_words(nc.sync, "w0_w", w0_words[0], R, U16)
         load_scales(nc.sync, w0_s, w0_scales)
         list5 = load_list("list5", offs5)
@@ -125,11 +125,12 @@ def tile_list_neighbours_bank_further_tabled_kernel(
 
         xt5_s = pick("xt5_s", xt_s, list5, U8)
         xt5_w = pick("xt5_w", xt_w, list5, U16)
-        p_ps = [ps.tile([P, O], F32, name=f"p_ps{m}") for m in range(2)]
-        for m in range(2):
-            rows = slice(m * P, (m + 1) * P)
-            nc.tensor.matmul_mx(p_ps[m][:], lhsT=ws_w[:, rows].bitcast(E4M3), lhsT_scale=ws_s[:, rows],
-                                rhs=xt5_w[:].bitcast(E2M1), rhs_scale=xt5_s[:], start=True, stop=False)
+        quarters = [(h, m) for h in (1, 0) for m in range(2)]
+        p_ps = {(h, m): ps.tile([P, HALF], F32, name=f"p_ps{h}{m}") for h, m in quarters}
+        for h, m in quarters:
+            rows, cols = slice(m * P, (m + 1) * P), slice(h * HALF, (h + 1) * HALF)
+            nc.tensor.matmul_mx(p_ps[h, m][:], lhsT=ws_w[:, rows].bitcast(E4M3), lhsT_scale=ws_s[:, rows],
+                                rhs=xt5_w[:, cols].bitcast(E2M1), rhs_scale=xt5_s[:, cols], start=True, stop=False)
 
         def scalar_copy(dst, src):
             nc.scalar.activation(dst, src, ACT.Copy)
@@ -139,7 +140,7 @@ def tile_list_neighbours_bank_further_tabled_kernel(
         ca = [new(f"ca{t}", [P, WINDOW], F32) for t in range(PACK)]
         cb = [new(f"cb{t}", [P, O], F32, tag=f"cb{t}") for t in range(PACK)]
         diff = new("diff", [P, PACK, O], F32)
-        hid = new("hid", [P, O, PACK], BF16)
+        hid = [new(f"hid{h}", [P, HALF, PACK], BF16) for h in range(2)]
 
         def evacuate(copy, t):
             copy(a_sb[t][:, :J], a_ps[t][:])
@@ -167,23 +168,23 @@ def tile_list_neighbours_bank_further_tabled_kernel(
             subtract(nc.vector, t)
         tz6 = [take_entries(0, "a3")]
 
-        woven = diff[:].rearrange("p t o -> p o t")
         nc.scalar.activation(
-            hid[:, :SCALAR_PLACES, :].rearrange("p (c i) t -> p c t i", i=4),
-            diff[:, :, :SCALAR_PLACES].rearrange("p t (c i) -> p c t i", i=4),
+            hid[0][:].rearrange("p (c i) t -> p c t i", i=4),
+            diff[:, :, :HALF].rearrange("p t (c i) -> p c t i", i=4),
             ACT.Abs,
         )
-        rest = woven[:, SCALAR_PLACES:, :]
-        nc.vector.scalar_tensor_tensor(hid[:, SCALAR_PLACES:, :], rest, -1.0, rest, ALU.mult, ALU.max)
+        woven = diff[:, :, HALF:].rearrange("p t o -> p o t")
+        nc.vector.scalar_tensor_tensor(hid[1][:], woven, -1.0, woven, ALU.mult, ALU.max)
         tz6.append(take_entries(1, "cb3"))
 
-        hid_w = new("hid_w", [P, O], U32)
-        hid_s = new("hid_s", [P, O], U8)
-        nc.vector.quantize_mx(hid_w[:].bitcast(E5M2), hid_s[:], hid[:].rearrange("p o t -> p (o t)"))
-        for m in range(2):
-            rows = slice(m * P, (m + 1) * P)
-            nc.tensor.matmul_mx(p_ps[m][:], lhsT=wb_w[:, rows].bitcast(E2M1), lhsT_scale=wb_s[:, rows],
-                                rhs=hid_w[:].bitcast(E5M2), rhs_scale=hid_s[:], start=False, stop=True)
-            res = new(f"res{m}", [P, O], F32)
-            nc.vector.tensor_tensor(res[:], p_ps[m][:], tz6[m][:], ALU.add)
-            nc.sync.dma_start(out[rows, :], res[:])
+        hid_w = [new(f"hid_w{h}", [P, HALF], U32) for h in range(2)]
+        hid_s = [new(f"hid_s{h}", [P, HALF], U8) for h in range(2)]
+        for h in (1, 0):
+            nc.vector.quantize_mx(hid_w[h][:].bitcast(E5M2), hid_s[h][:], hid[h][:].rearrange("p o t -> p (o t)"))
+        for h, m in quarters:
+            rows, cols = slice(m * P, (m + 1) * P), slice(h * HALF, (h + 1) * HALF)
+            nc.tensor.matmul_mx(p_ps[h, m][:], lhsT=wb_w[:, rows].bitcast(E2M1), lhsT_scale=wb_s[:, rows],
+                                rhs=hid_w[h][:].bitcast(E5M2), rhs_scale=hid_s[h][:], start=False, stop=True)
+            res = new(f"res{h}{m}", [P, HALF], F32)
+            nc.vector.tensor_tensor(res[:], p_ps[h, m][:], tz6[m][:, cols], ALU.add)
+            nc.sync.dma_start(out[rows, cols], res[:])

from contextlib import ExitStack

import concourse.mybir as mybir

F32 = mybir.dt.float32
BF16 = mybir.dt.bfloat16
I32 = mybir.dt.int32
U32 = mybir.dt.uint32
U16 = mybir.dt.uint16
U8 = mybir.dt.uint8
E4M3 = mybir.dt.float8_e4m3fn_x4
E5M2 = mybir.dt.float8_e5m2_x4
E2M1 = mybir.dt.float4_e2m1fn_x4
ALU = mybir.AluOpType
ACT = mybir.ActivationFunctionType

P = 128
PACK = 4
K, T, Z, J, R, O, N, E = 512, 1024, 1024, 256, 512, 256, 256, 1024
FLOPS = 2 * (2 * K * R * J + R * N * O + K * N * O)
WINDOW = 352
HALF = O // 2


def tile_list_neighbours_bank_further_tabled_kernel(
    tc, xt_words, xt_scales, w_words, w_scales, xo_words, xo_scales, w0_words, w0_scales,
    wb_words, wb_scales, ws_words, ws_scales, tz, offs, offs2, offs3, offs4, offs5, offs6, out,
):
    nc = tc.nc
    with ExitStack() as ctx:
        sb = ctx.enter_context(tc.tile_pool(name="sb", bufs=1))
        ps = ctx.enter_context(tc.psum_pool(name="ps", bufs=1))

        def new(name, shape, dtype, tag=""):
            return sb.tile(shape, dtype, name=name, tag=tag, align_bytes=64)

        def load_list(name, src):
            tile = sb.tile([P, 16], U16, name=name)
            nc.sync.dma_start(tile[:], src)
            return tile

        def load_words(queue, name, src, cols, dtype):
            tile = new(name, [P, cols], dtype)
            queue.dma_start(tile[:].bitcast(I32), src.bitcast(I32))
            return tile

        def load_scales(queue, tile, src, quadrants=range(4)):
            for q in quadrants:
                queue.dma_start(tile[32 * q : 32 * q + 4, :].bitcast(I32), src[0, 4 * q : 4 * q + 4, :].bitcast(I32))

        def load_scales_repeated(queue, tile, src, quadrants=range(4)):
            for q in quadrants:
                rows = src[0, 4 * q : 4 * q + 4, :].bitcast(I32)
                queue.dma_start(tile[32 * q : 32 * q + 32, :].bitcast(I32), rows.unsqueeze(0).broadcast_to([8] + list(rows.shape)))

        def zeroed_plane(name, cols):
            tile = new(name, [P, cols], U8)
            nc.vector.memset(tile[:].bitcast(I32), 0)
            return tile

        xt_s, xo_s = new("xt_s", [P, T], U8), new("xo_s", [P, Z], U8)
        w_s, w0_s = zeroed_plane("w_s", R), zeroed_plane("w0_s", R)
        ws_s, wb_s = zeroed_plane("ws_s", N), zeroed_plane("wb_s", N)

        def fp8_rows(words):
            return words[0].rearrange("p n t -> p (n t)")

        def load_tz(m):
            tile = new(f"tz{m}", [P, E], F32)
            nc.sync.dma_start(tile[:], tz[m * P : (m + 1) * P, :])
            return tile

        xo_w = load_words(nc.gpsimd, "xo_w", fp8_rows(xo_words), Z, U32)
        w_w = load_words(nc.gpsimd, "w_w", fp8_rows(w_words), R, U32)
        load_scales_repeated(nc.gpsimd, xo_s, xo_scales, range(1))
        list1 = load_list("list1", offs)
        load_scales_repeated(nc.scalar, xt_s, xt_scales, range(3))
        load_scales_repeated(nc.sync, xt_s, xt_scales, range(3, 4))
        xt_w = load_words(nc.sync, "xt_w", xt_words[0], T, U16)
        list2 = load_list("list2", offs2)
        load_scales(nc.sync, w_s, w_scales)
        load_scales_repeated(nc.sync, xo_s, xo_scales, range(1, 4))
        w0_w = load_words(nc.sync, "w0_w", w0_words[0], R, U16)
        load_scales(nc.sync, w0_s, w0_scales)
        list5 = load_list("list5", offs5)
        list3 = load_list("list3", offs3)
        tz_sb = [load_tz(0)]
        list4 = load_list("list4", offs4)
        list6 = load_list("list6", offs6)
        ws_w = load_words(nc.sync, "ws_w", fp8_rows(ws_words), N, U32)
        wb_w = load_words(nc.sync, "wb_w", wb_words[0], N, U16)
        load_scales(nc.sync, ws_s, ws_scales)
        tz_sb.append(load_tz(1))
        load_scales(nc.sync, wb_s, wb_scales)

        def deal(engine_copy, name, src, dtype, line):
            dealt = new(name, [P, PACK, P], dtype)
            engine_copy(
                dealt[:].rearrange("p t (c i) -> p c t i", i=line),
                src[:].rearrange("p (c i t) -> p c t i", i=line, t=PACK),
            )
            return dealt

        def pick(name, src, offsets, dtype):
            picked = new(name, [P, J], dtype)
            nc.vector.tensor_copy(picked[:], src[:].indirect(offsets[:]))
            return picked

        xt1_s = pick("xt1_s", xt_s, list1, U8)
        xt1_w = pick("xt1_w", xt_w, list1, U16)
        w_sd = deal(nc.vector.tensor_copy, "w_sd", w_s, U8, 16)
        w_wd = deal(nc.scalar.copy, "w_wd", w_w, U32, 4)
        w0_wd = deal(nc.scalar.copy, "w0_wd", w0_w, U16, 8)
        xo2_w = pick("xo2_w", xo_w, list2, U32)
        xo2_s = pick("xo2_s", xo_s, list2, U8)
        w0_sd = deal(nc.vector.tensor_copy, "w0_sd", w0_s, U8, 16)

        a_ps = [ps.tile([P, J], F32, name=f"a_ps{t}") for t in range(PACK)]
        for t in range(PACK):
            nc.tensor.matmul_mx(a_ps[t][:], lhsT=w_wd[:, t, :].bitcast(E4M3), lhsT_scale=w_sd[:, t, :],
                                rhs=xt1_w[:].bitcast(E2M1), rhs_scale=xt1_s[:], start=True, stop=False)
        for t in range(PACK):
            nc.tensor.matmul_mx(a_ps[t][:], lhsT=w0_wd[:, t, :].bitcast(E2M1), lhsT_scale=w0_sd[:, t, :],
                                rhs=xo2_w[:].bitcast(E4M3), rhs_scale=xo2_s[:], start=False, stop=True)

        xt5_s = pick("xt5_s", xt_s, list5, U8)
        xt5_w = pick("xt5_w", xt_w, list5, U16)
        quarters = [(h, m) for h in (1, 0) for m in range(2)]
        p_ps = {(h, m): ps.tile([P, HALF], F32, name=f"p_ps{h}{m}") for h, m in quarters}
        for h, m in quarters:
            rows, cols = slice(m * P, (m + 1) * P), slice(h * HALF, (h + 1) * HALF)
            nc.tensor.matmul_mx(p_ps[h, m][:], lhsT=ws_w[:, rows].bitcast(E4M3), lhsT_scale=ws_s[:, rows],
                                rhs=xt5_w[:, cols].bitcast(E2M1), rhs_scale=xt5_s[:, cols], start=True, stop=False)

        def scalar_copy(dst, src):
            nc.scalar.activation(dst, src, ACT.Copy)

        vector_copy = nc.vector.tensor_copy
        a_sb = [new(f"a{t}", [P, WINDOW], F32, tag=f"a{t}") for t in range(PACK)]
        ca = [new(f"ca{t}", [P, WINDOW], F32) for t in range(PACK)]
        cb = [new(f"cb{t}", [P, O], F32, tag=f"cb{t}") for t in range(PACK)]
        diff = new("diff", [P, PACK, O], F32)
        hid = [new(f"hid{h}", [P, HALF, PACK], BF16) for h in range(2)]

        def evacuate(copy, t):
            copy(a_sb[t][:, :J], a_ps[t][:])

        def take_slots(copy, t):
            copy(ca[t][:, :O], a_sb[t][:].indirect(list3[:]))

        def take_neighbours(copy, t):
            copy(cb[t][:], ca[t][:].indirect(list4[:]))

        def subtract(engine, t):
            engine.tensor_tensor(diff[:, t, :], ca[t][:, :O], cb[t][:], ALU.subtract)

        def take_entries(m, tag):
            taken = new(f"tz6_{m}", [P, O], F32, tag=tag)
            scalar_copy(taken[:], tz_sb[m][:].indirect(list6[:]))
            return taken

        for t in range(PACK):
            evacuate(scalar_copy, t)
        for take in (take_slots, take_neighbours):
            for t in range(PACK):
                take(vector_copy if t < 2 else scalar_copy, t)
        for t in range(PACK):
            subtract(nc.vector, t)
        tz6 = [take_entries(0, "a3")]

        nc.scalar.activation(
            hid[0][:].rearrange("p (c i) t -> p c t i", i=4),
            diff[:, :, :HALF].rearrange("p t (c i) -> p c t i", i=4),
            ACT.Abs,
        )
        woven = diff[:, :, HALF:].rearrange("p t o -> p o t")
        nc.vector.scalar_tensor_tensor(hid[1][:], woven, -1.0, woven, ALU.mult, ALU.max)
        tz6.append(take_entries(1, "cb3"))

        hid_w = [new(f"hid_w{h}", [P, HALF], U32) for h in range(2)]
        hid_s = [new(f"hid_s{h}", [P, HALF], U8) for h in range(2)]
        for h in (1, 0):
            nc.vector.quantize_mx(hid_w[h][:].bitcast(E5M2), hid_s[h][:], hid[h][:].rearrange("p o t -> p (o t)"))
        for h, m in quarters:
            rows, cols = slice(m * P, (m + 1) * P), slice(h * HALF, (h + 1) * HALF)
            nc.tensor.matmul_mx(p_ps[h, m][:], lhsT=wb_w[:, rows].bitcast(E2M1), lhsT_scale=wb_s[:, rows],
                                rhs=hid_w[h][:].bitcast(E5M2), rhs_scale=hid_s[h][:], start=False, stop=True)
            res = new(f"res{h}{m}", [P, HALF], F32)
            nc.vector.tensor_tensor(res[:], p_ps[h, m][:], tz6[m][:, cols], ALU.add)
            nc.sync.dma_start(out[rows, cols], res[:])
